import numpy as np
import ml_dtypes

BF16 = ml_dtypes.bfloat16


def bf(x):
    return np.asarray(x, np.float32).astype(BF16)


def f32(x):
    return np.asarray(x, np.float32)


def f64(x):
    return np.asarray(x).astype(np.float64)


def striped(idx):
    return np.tile(idx.reshape(-1, 16).T, (8, 1))


def rows(idx, k):
    return np.tile(idx, (k, 1))


def look(tab, idx):
    return np.take_along_axis(f64(tab), rows(idx, len(tab)), axis=1)


K, S, V, N, M = 128, 2048, 2048, 2048, 128


def setup_inputs():
    return {"tab": f32(np.random.standard_normal((2, K, S))), "y": f32(np.random.standard_normal((K, V))), "w": bf(np.random.standard_normal((K, M)) / np.sqrt(K)), "b": f32(0.5 * np.random.standard_normal((M, 1))), "offs": striped(np.random.permutation(S)[:N])}


def reference(tab, y, w, b, offs):
    idx = offs[:16].T.reshape(-1)
    x = (look(tab[0], idx) * f64(y)) * (np.maximum(look(tab[1], idx), 0.0))
    return np.maximum(f64(w).T @ x + f64(b), 0.0)

@@ -1,0 +1,48 @@
+import concourse.mybir as mybir
+
+F32, BF16, U16 = mybir.dt.float32, mybir.dt.bfloat16, mybir.dt.uint16
+MULT = mybir.AluOpType.mult
+RELU = mybir.ActivationFunctionType.Relu
+
+ROWS, PLACES, N, M = 128, 2048, 2048, 128
+PIECE = 512
+PER_COLUMN = 16
+FLOPS = 2 * ROWS * M * N
+
+
+def tile_lookup_vg_mulrelu_relu_kernel(tc, tab, y, w, b, offs, out):
+    nc = tc.nc
+    pieces = N // PIECE
+    with (
+        tc.tile_pool(name="held", bufs=1) as held,
+        tc.tile_pool(name="work", bufs=pieces) as work,
+        tc.psum_pool(name="psum", bufs=pieces) as psum,
+    ):
+        offsets = held.tile([ROWS, N // PER_COLUMN], U16, name="offsets")
+        values = held.tile([ROWS, PLACES], F32, name="values")
+        gates = held.tile([ROWS, PLACES], F32, name="gates")
+        weights = held.tile([ROWS, M], BF16, name="weights")
+        bias = held.tile([M, 1], F32, name="bias")
+        streams = [work.tile([ROWS, PIECE], F32, name="stream") for p in range(pieces)]
+
+        nc.sync.dma_start(offsets[:], offs)
+        nc.sync.dma_start(gates[:], tab[1])
+        nc.sync.dma_start(values[:], tab[0])
+        for p in range(pieces):
+            nc.sync.dma_start(streams[p][:], y[:, p * PIECE:(p + 1) * PIECE])
+        nc.sync.dma_start(weights[:], w)
+        nc.sync.dma_start(bias[:], b)
+
+        for p in range(pieces):
+            entries = offsets[:, p * PIECE // PER_COLUMN:(p + 1) * PIECE // PER_COLUMN]
+            gate = work.tile([ROWS, PIECE], F32, name="gate")
+            nc.scalar.activation(gate[:], gates[:].indirect(entries), RELU)
+            scaled = work.tile([ROWS, PIECE], F32, name="scaled")
+            nc.vector.tensor_tensor(scaled[:], values[:].indirect(entries), streams[p][:], MULT)
+            x = work.tile([ROWS, PIECE], BF16, name="x")
+            nc.vector.tensor_tensor(x[:], scaled[:], gate[:], MULT)
+            product = psum.tile([M, PIECE], F32, name="product")
+            nc.tensor.matmul(product[:], weights[:], x[:], start=True, stop=True)
+            result = work.tile([M, PIECE], F32, name="result")
+            nc.scalar.activation(result[:], product[:], RELU, bias=bias[:])
+            nc.sync.dma_start(out[:, p * PIECE:(p + 1) * PIECE], result[:])

@@ -1,48 +1,77 @@
 import concourse.mybir as mybir
 
 F32, BF16, U16 = mybir.dt.float32, mybir.dt.bfloat16, mybir.dt.uint16
-MULT = mybir.AluOpType.mult
+MULT, ADD, MAX = mybir.AluOpType.mult, mybir.AluOpType.add, mybir.AluOpType.max
 RELU = mybir.ActivationFunctionType.Relu
 
 ROWS, PLACES, N, M = 128, 2048, 2048, 128
-PIECE = 512
 PER_COLUMN = 16
+PIECE = 256
+WIDTHS = [PIECE] * (N // PIECE - 1) + [PIECE // 2] * 2
+CHUNK = 512
+LATE = 2
+LAG = 2
+BANKS = 8
 FLOPS = 2 * ROWS * M * N
 
 
 def tile_lookup_vg_mulrelu_relu_kernel(tc, tab, y, w, b, offs, out):
     nc = tc.nc
-    pieces = N // PIECE
+    pieces = [slice(sum(WIDTHS[:p]), sum(WIDTHS[:p + 1])) for p in range(len(WIDTHS))]
     with (
         tc.tile_pool(name="held", bufs=1) as held,
-        tc.tile_pool(name="work", bufs=pieces) as work,
-        tc.psum_pool(name="psum", bufs=pieces) as psum,
+        tc.psum_pool(name="psum", bufs=BANKS) as psum,
     ):
         offsets = held.tile([ROWS, N // PER_COLUMN], U16, name="offsets")
         values = held.tile([ROWS, PLACES], F32, name="values")
         gates = held.tile([ROWS, PLACES], F32, name="gates")
         weights = held.tile([ROWS, M], BF16, name="weights")
         bias = held.tile([M, 1], F32, name="bias")
-        streams = [work.tile([ROWS, PIECE], F32, name="stream") for p in range(pieces)]
+        stream = held.tile([ROWS, N], F32, name="stream")
+        scaled = held.tile([ROWS, N], F32, name="scaled")
+        gated = held.tile([ROWS, N], F32, name="gated")
+        x = held.tile([ROWS, N], BF16, name="x")
+        result = held.tile([M, N], F32, name="result")
+
+        warm_in = held.tile([ROWS, 8], F32, name="warm_in")
+        warm_out = held.tile([ROWS, 8], F32, name="warm_out")
+        nc.vector.memset(warm_in[:], 0.0)
+        nc.scalar.activation(warm_out[:], warm_in[:], RELU)
 
         nc.sync.dma_start(offsets[:], offs)
-        nc.sync.dma_start(gates[:], tab[1])
         nc.sync.dma_start(values[:], tab[0])
-        for p in range(pieces):
-            nc.sync.dma_start(streams[p][:], y[:, p * PIECE:(p + 1) * PIECE])
+        for start in range(LATE * PIECE, N, CHUNK):
+            nc.sync.dma_start(stream[:, start:start + CHUNK], y[:, start:start + CHUNK])
+        nc.sync.dma_start(gates[:], tab[1])
+        nc.sync.dma_start(stream[:, :CHUNK], y[:, :CHUNK])
         nc.sync.dma_start(weights[:], w)
         nc.sync.dma_start(bias[:], b)
 
-        for p in range(pieces):
-            entries = offsets[:, p * PIECE // PER_COLUMN:(p + 1) * PIECE // PER_COLUMN]
-            gate = work.tile([ROWS, PIECE], F32, name="gate")
-            nc.scalar.activation(gate[:], gates[:].indirect(entries), RELU)
-            scaled = work.tile([ROWS, PIECE], F32, name="scaled")
-            nc.vector.tensor_tensor(scaled[:], values[:].indirect(entries), streams[p][:], MULT)
-            x = work.tile([ROWS, PIECE], BF16, name="x")
-            nc.vector.tensor_tensor(x[:], scaled[:], gate[:], MULT)
-            product = psum.tile([M, PIECE], F32, name="product")
-            nc.tensor.matmul(product[:], weights[:], x[:], start=True, stop=True)
-            result = work.tile([M, PIECE], F32, name="result")
-            nc.scalar.activation(result[:], product[:], RELU, bias=bias[:])
-            nc.sync.dma_start(out[:, p * PIECE:(p + 1) * PIECE], result[:])
+        def entries(piece):
+            return offsets[:, piece.start // PER_COLUMN:piece.stop // PER_COLUMN]
+
+        for piece in pieces[LATE:] + pieces[:LATE]:
+            nc.vector.tensor_tensor(scaled[:, piece], values[:].indirect(entries(piece)), stream[:, piece], MULT)
+
+        def finish_on_vector(p):
+            nc.vector.tensor_scalar(result[:, pieces[p]], products[p][:], bias[:], 0.0, ADD, MAX)
+            nc.sync.dma_start(out[:, pieces[p]], result[:, pieces[p]])
+
+        def finish_on_scalar(p):
+            nc.scalar.activation(result[:, pieces[p]], products[p][:], RELU, bias=bias[:])
+            nc.sync.dma_start(out[:, pieces[p]], result[:, pieces[p]])
+
+        early = N // 2 // PIECE
+        products = []
+        for p, piece in enumerate(pieces):
+            nc.scalar.activation(gated[:, piece], gates[:].indirect(entries(piece)), RELU)
+            nc.vector.tensor_tensor(x[:, piece], scaled[:, piece], gated[:, piece], MULT)
+            products.append(psum.tile([M, WIDTHS[p]], F32, name="product"))
+            nc.tensor.matmul(products[p][:], weights[:], x[:, piece], start=True, stop=True)
+            if LAG <= p < LAG + early:
+                finish_on_vector(p - LAG)
+        for p in range(early, len(pieces)):
+            if WIDTHS[p] == PIECE:
+                finish_on_scalar(p)
+            else:
+                finish_on_vector(p)

import concourse.mybir as mybir

F32, BF16, U16 = mybir.dt.float32, mybir.dt.bfloat16, mybir.dt.uint16
MULT, ADD, MAX = mybir.AluOpType.mult, mybir.AluOpType.add, mybir.AluOpType.max
RELU = mybir.ActivationFunctionType.Relu

ROWS, PLACES, N, M = 128, 2048, 2048, 128
PER_COLUMN = 16
PIECE = 256
WIDTHS = [PIECE] * (N // PIECE - 1) + [PIECE // 2] * 2
CHUNK = 512
LATE = 2
LAG = 2
BANKS = 8
FLOPS = 2 * ROWS * M * N


def tile_lookup_vg_mulrelu_relu_kernel(tc, tab, y, w, b, offs, out):
    nc = tc.nc
    pieces = [slice(sum(WIDTHS[:p]), sum(WIDTHS[:p + 1])) for p in range(len(WIDTHS))]
    with (
        tc.tile_pool(name="held", bufs=1) as held,
        tc.psum_pool(name="psum", bufs=BANKS) as psum,
    ):
        offsets = held.tile([ROWS, N // PER_COLUMN], U16, name="offsets")
        values = held.tile([ROWS, PLACES], F32, name="values")
        gates = held.tile([ROWS, PLACES], F32, name="gates")
        weights = held.tile([ROWS, M], BF16, name="weights")
        bias = held.tile([M, 1], F32, name="bias")
        stream = held.tile([ROWS, N], F32, name="stream")
        scaled = held.tile([ROWS, N], F32, name="scaled")
        gated = held.tile([ROWS, N], F32, name="gated")
        x = held.tile([ROWS, N], BF16, name="x")
        result = held.tile([M, N], F32, name="result")

        warm_in = held.tile([ROWS, 8], F32, name="warm_in")
        warm_out = held.tile([ROWS, 8], F32, name="warm_out")
        nc.vector.memset(warm_in[:], 0.0)
        nc.scalar.activation(warm_out[:], warm_in[:], RELU)

        nc.sync.dma_start(offsets[:], offs)
        nc.sync.dma_start(values[:], tab[0])
        for start in range(LATE * PIECE, N, CHUNK):
            nc.sync.dma_start(stream[:, start:start + CHUNK], y[:, start:start + CHUNK])
        nc.sync.dma_start(gates[:], tab[1])
        nc.sync.dma_start(stream[:, :CHUNK], y[:, :CHUNK])
        nc.sync.dma_start(weights[:], w)
        nc.sync.dma_start(bias[:], b)

        def entries(piece):
            return offsets[:, piece.start // PER_COLUMN:piece.stop // PER_COLUMN]

        for piece in pieces[LATE:] + pieces[:LATE]:
            nc.vector.tensor_tensor(scaled[:, piece], values[:].indirect(entries(piece)), stream[:, piece], MULT)

        def finish_on_vector(p):
            nc.vector.tensor_scalar(result[:, pieces[p]], products[p][:], bias[:], 0.0, ADD, MAX)
            nc.sync.dma_start(out[:, pieces[p]], result[:, pieces[p]])

        def finish_on_scalar(p):
            nc.scalar.activation(result[:, pieces[p]], products[p][:], RELU, bias=bias[:])
            nc.sync.dma_start(out[:, pieces[p]], result[:, pieces[p]])

        early = N // 2 // PIECE
        products = []
        for p, piece in enumerate(pieces):
            nc.scalar.activation(gated[:, piece], gates[:].indirect(entries(piece)), RELU)
            nc.vector.tensor_tensor(x[:, piece], scaled[:, piece], gated[:, piece], MULT)
            products.append(psum.tile([M, WIDTHS[p]], F32, name="product"))
            nc.tensor.matmul(products[p][:], weights[:], x[:, piece], start=True, stop=True)
            if LAG <= p < LAG + early:
                finish_on_vector(p - LAG)
        for p in range(early, len(pieces)):
            if WIDTHS[p] == PIECE:
                finish_on_scalar(p)
            else:
                finish_on_vector(p)
